import numpy as np
import ml_dtypes


def mxq(x, axis, fmt="e4m3"):
    dtype, down = {"e4m3": (ml_dtypes.float8_e4m3fn, 7), "e5m2": (ml_dtypes.float8_e5m2, 14)}[fmt]
    v = np.moveaxis(np.asarray(x, np.float32).astype(ml_dtypes.bfloat16).astype(np.float64), axis, -1)
    blocks = v.reshape(v.shape[:-1] + (-1, 32))
    amax = np.abs(blocks).max(-1, keepdims=True)
    byte = np.maximum(np.where(amax > 0, np.frexp(amax)[1] - 1 + 127, 0) - down, 1)
    scale = np.exp2(byte - 127.0)
    codes = (blocks / scale).astype(np.float32).astype(dtype).astype(np.float64)
    return np.moveaxis((codes * scale).reshape(v.shape), -1, axis)


WIDE = False


def mx_kscale(k):
    if not WIDE:
        return np.ones(k)
    levels = np.array([10, -10, 5, -5, 0])
    if k % 512:
        return np.exp2(np.random.permutation(np.resize(levels, k // 32))).repeat(32)
    a = np.empty((k // 512, 16))
    for p in range(k // 512):
        a[p, :8] = np.random.permutation(np.resize(levels, 8))
        for g in range(8):
            far = levels[np.abs(levels - a[p, g]) >= 10]
            a[p, g + 8] = far[np.random.randint(len(far))]
    return np.exp2(a.ravel()).repeat(32)


def f64(x):
    return np.asarray(x).astype(np.float64)


def striped8(idx):
    return np.asarray(idx).reshape(8, -1, 16).transpose(0, 2, 1).reshape(128, -1).astype(np.uint16)


def unstriped8(offs):
    return offs.reshape(8, 16, -1).transpose(0, 2, 1).reshape(8, -1).astype(np.int64)


def pick8(x, idx, run):
    r = np.arange(len(x))
    return x[r[:, None], idx[r % (8 * run) // run]]


E2M1 = np.array([0.0, 0.5, 1.0, 1.5, 2.0, 3.0, 4.0, 6.0, -0.0, -0.5, -1.0, -1.5, -2.0, -3.0, -4.0, -6.0])


def pack_weight(w, fmt):
    k, n = w.shape
    w = f64(np.asarray(w, np.float32).astype(ml_dtypes.bfloat16)).reshape(k // 32, 32, n)
    amax = np.abs(w).max(1)
    if fmt == "e4m3":
        byte = np.frexp(amax)[1] - 1 + 127 - 7
    else:
        mant, ex = np.frexp(amax / 6.0)
        byte = np.where(mant > 0.5, ex, ex - 1) + 127
    byte = np.clip(np.where(amax > 0, byte, 1), 1, 254)
    scaled = (w * np.exp2(127.0 - byte)[:, None, :]).reshape(k, n).astype(np.float32)
    by_word = np.ascontiguousarray(scaled.reshape(k // 512, 128, 4, n).transpose(0, 1, 3, 2))
    if fmt == "e4m3":
        words = by_word.astype(ml_dtypes.float8_e4m3fn).view(np.uint8)
    else:
        c = by_word.astype(ml_dtypes.float4_e2m1fn).view(np.uint8) & 0xF
        words = (c[..., 0::2] | (c[..., 1::2] << 4)).reshape(k // 512, 128, 2 * n)
    return np.ascontiguousarray(words), np.ascontiguousarray(byte.astype(np.uint8).reshape(k // 512, 16, n))


def unpack_weight(words, scales, fmt):
    g, _, n = scales.shape
    words = np.ascontiguousarray(words).reshape(g, 128, n, -1)
    if fmt == "e4m3":
        vals = words.view(ml_dtypes.float8_e4m3fn).astype(np.float64)
    else:
        nib = np.empty((g, 128, n, 4), np.uint8)
        nib[..., 0::2] = words & 0xF
        nib[..., 1::2] = words >> 4
        vals = E2M1[nib]
    vals = vals * np.repeat(np.exp2(scales.astype(np.float64) - 127.0), 8, axis=1)[..., None]
    return vals.transpose(0, 1, 3, 2).reshape(g * 512, n)


def sigmoid(v):
    return 1.0 / (1.0 + np.exp(-v))


D, V, Q, I = 512, 2048, 128, 512


def setup_inputs():
    n = np.random.standard_normal
    idx = np.stack([np.random.permutation(V)[:I] for _ in range(8)])
    idx2 = np.stack([np.random.permutation(V)[:I] for _ in range(8)])
    fd = mx_kscale(D)
    vocp = pack_weight(n((D, V)) / fd[:, None], "e2m1")
    return {
        "hid": (n((D, Q)) * 1.0 / np.sqrt(D) * fd[:, None]).astype(np.float32),
        "voc_words": vocp[0],
        "voc_scales": vocp[1],
        "margin": (np.random.uniform(0.0, 1.0, (1, I))).astype(np.float32),
        "steep": (np.random.uniform(1.0, 3.0, (Q, 1))).astype(np.float32),
        "old": (0.5 * n((Q, V))).astype(np.float32),
        "offs": striped8(idx),
        "offs2": striped8(idx2),
    }


def reference(hid, voc_words, voc_scales, margin, steep, old, offs, offs2):
    idx = unstriped8(offs)
    idx2 = unstriped8(offs2)
    vocu = unpack_weight(voc_words, voc_scales, "e2m1")
    hidq = mxq(f64(hid), 0, "e4m3")
    a = hidq.T @ vocu
    b = pick8(a, idx2, 16) - pick8(a, idx, 16)
    db = sigmoid((b + f64(margin)) * f64(steep)) * f64(steep)
    s1 = np.zeros((Q, V))
    s1[np.arange(Q)[:, None], idx2[np.arange(Q) % 128 // 16]] = db
    e2 = db * (-1.0)
    s2 = np.zeros((Q, V))
    s2[np.arange(Q)[:, None], idx[np.arange(Q) % 128 // 16]] = e2
    da = s1 + s2
    y = da + f64(old)
    return y

@@ -1,0 +1,172 @@
+from contextlib import ExitStack
+
+import concourse.mybir as mybir
+from concourse.masks import make_identity
+
+D, V, Q, I = 512, 2048, 128, 512
+FLOPS = 2 * D * V * Q
+
+F32 = mybir.dt.float32
+BF16 = mybir.dt.bfloat16
+I32 = mybir.dt.int32
+U32 = mybir.dt.uint32
+U16 = mybir.dt.uint16
+U8 = mybir.dt.uint8
+FP8X4 = mybir.dt.float8_e4m3fn_x4
+FP4X4 = mybir.dt.float4_e2m1fn_x4
+ALU = mybir.AluOpType
+ACT = mybir.ActivationFunctionType
+
+P = 128
+PACK = 4
+BANK = 512
+SCORE_WIDTHS = (512, 512, 512, 256, 128, 128)
+FIRST = 128
+OUT_WIDTH = 256
+
+
+def tile_attend_bpairmargin_heads_kernel(tc, hid, voc_words, voc_scales, margin, steep, old, offs, offs2, out):
+    nc = tc.nc
+    with ExitStack() as ctx:
+        keep = ctx.enter_context(tc.tile_pool(name="keep", bufs=1))
+        psum = ctx.enter_context(tc.psum_pool(name="psum", bufs=1))
+
+        plane = keep.tile([P, V], U8, name="plane", align_bytes=64)
+        nc.vector.memset(plane[:].bitcast(I32), 0)
+        warm = keep.tile([P, 2], F32, name="warm")
+        nc.gpsimd.memset(warm[:, 0:1], 0.0)
+
+        raw = keep.tile([P, PACK, Q], F32, name="raw")
+        mcol = keep.tile([P, PACK], F32, name="mcol", tag="codes", align_bytes=64)
+        nc.sync.dma_start(out=mcol[:], in_=margin.rearrange("o (p j) -> (o p) j", j=PACK))
+        nc.sync.dma_start(out=raw[:], in_=hid.rearrange("(p t) q -> p t q", t=PACK))
+        nc.scalar.activation(out=warm[:, 1:2], in_=warm[:, 0:1], func=ACT.Sigmoid)
+        scale_rows = voc_scales[0].bitcast(I32).rearrange("(g r) c -> r g c", r=4)
+        halves = []
+        for h in range(2):
+            words = keep.tile([P, V], U8, name=f"words{h}", tag=f"words{h}", align_bytes=64)
+            nc.sync.dma_start(out=words[:].bitcast(I32), in_=voc_words[0].bitcast(I32)[:, h * 512 : (h + 1) * 512])
+            halves.append(words)
+            if h == 0:
+                for r in range(4):
+                    nc.sync.dma_start(out=plane[:].bitcast(I32)[r:P:32, :], in_=scale_rows[r])
+        list1 = keep.tile([P, I // 16], U16, name="list1")
+        nc.sync.dma_start(list1[:], offs)
+        list2 = keep.tile([P, I // 16], U16, name="list2")
+        nc.sync.dma_start(list2[:], offs2)
+        steep_col = keep.tile([P, 1], F32, name="steep_col")
+        nc.sync.dma_start(out=steep_col[:], in_=steep)
+        olds = []
+        for b in range(4):
+            old_b = keep.tile([P, BANK], F32, name=f"old{b}")
+            nc.sync.dma_start(out=old_b[:], in_=old[:, b * BANK : (b + 1) * BANK])
+            olds.append(old_b)
+
+        ident = keep.tile([P, P], F32, name="ident")
+        make_identity(nc, ident[:])
+        s1 = keep.tile([P, V], F32, name="s1")
+        nc.vector.memset(s1[:], 0.0)
+
+        mbank = psum.tile([P, PACK, P], F32, name="mbank", tag="bank6")
+        for j in range(PACK):
+            nc.tensor.transpose(mbank[:, j, :], mcol[:, j : j + 1].to_broadcast([P, P]), ident[:])
+        margin_row = keep.tile([P, I], F32, name="margin_row")
+        nc.scalar.copy(out=margin_row[:].rearrange("p (n j) -> p n j", j=PACK), in_=mbank[:].rearrange("p j n -> p n j"))
+
+        grouped = keep.tile([P, Q, PACK], BF16, name="grouped", tag="late_zero", align_bytes=64)
+        codes = keep.tile([P, Q], U32, name="codes", tag="codes", align_bytes=64)
+        hscale = keep.tile([P, Q], U8, name="hscale", align_bytes=64)
+        for h in range(2):
+            cols = slice(h * 64, (h + 1) * 64)
+            nc.vector.tensor_copy(out=grouped[:, cols, :], in_=raw[:, :, cols].rearrange("p t q -> p q t"))
+        for h in range(2):
+            cols = slice(h * 64, (h + 1) * 64)
+            nc.vector.quantize_mx(
+                out=codes[:, cols].bitcast(FP8X4),
+                scales=hscale[:, cols],
+                in_=grouped[:, cols, :].rearrange("p q t -> p (q t)"),
+            )
+        s2 = keep.tile([P, V], F32, name="s2", tag="late_zero", align_bytes=64)
+        nc.gpsimd.memset(s2[:], 0.0)
+
+        scores = keep.tile([P, V], F32, name="scores")
+        c0 = 0
+        for n, width in enumerate(SCORE_WIDTHS):
+            acc = psum.tile([P, width], F32, name=f"acc{n}", tag=f"bank{n}")
+            words = halves[c0 // 1024]
+            w0 = 2 * (c0 % 1024)
+            nc.tensor.matmul_mx(
+                out=acc[:],
+                lhsT=codes[:].bitcast(FP8X4),
+                lhsT_scale=hscale[:],
+                rhs=words[:, w0 : w0 + 2 * width].bitcast(FP4X4),
+                rhs_scale=plane[:, c0 : c0 + width],
+                start=True,
+                stop=True,
+            )
+            if n % 2 == 0:
+                nc.vector.tensor_copy(out=scores[:, c0 : c0 + width], in_=acc[:])
+            else:
+                nc.scalar.copy(out=scores[:, c0 : c0 + width], in_=acc[:])
+            c0 = c0 + width
+
+        steep_rows = keep.tile([P, I], F32, name="steep_rows", tag="words1", align_bytes=64)
+        nc.scalar.activation(out=steep_rows[:], in_=steep_col[:].to_broadcast([P, I]), func=ACT.Copy)
+        minus_rows = keep.tile([P, FIRST], F32, name="minus_rows")
+        nc.scalar.activation(out=minus_rows[:], in_=steep_rows[:, 0:FIRST], func=ACT.Copy, scale=-1.0)
+
+        turned = []
+        for b in range(3):
+            tb = psum.tile([P, 4, P], F32, name=f"turned{b}", tag=f"bank{b}")
+            for j in range(4):
+                nc.tensor.matmul(tb[:, j, :], lhsT=olds[b][:, j * P : (j + 1) * P], rhs=ident[:],
+                                 start=(j == 0), stop=False, is_transpose=True)
+            turned.append(tb)
+
+        lower = keep.tile([P, I], F32, name="lower")
+        nc.vector.tensor_tensor(lower[:], scores[:].indirect(list1[:]), margin_row[:], ALU.subtract)
+        gap = keep.tile([P, I], F32, name="gap")
+        nc.vector.tensor_tensor(gap[:], scores[:].indirect(list2[:]), lower[:], ALU.subtract)
+        sig = keep.tile([P, I], F32, name="sig")
+        for lo, hi in ((0, FIRST), (FIRST, I)):
+            nc.scalar.activation(out=sig[:, lo:hi], in_=gap[:, lo:hi], func=ACT.Sigmoid, scale=steep_col[:])
+        e2 = keep.tile([P, I - FIRST], F32, name="e2")
+        nc.scalar.activation(out=e2[:], in_=sig[:, FIRST:I], func=ACT.Copy, scale=minus_rows[:, 0:1])
+        nc.vector.tensor_tensor(s2[:].indirect(list1[:, 0 : FIRST // 16]), sig[:, 0:FIRST], minus_rows[:], ALU.mult)
+        nc.vector.tensor_tensor(s1[:].indirect(list2[:]), sig[:], steep_rows[:], ALU.mult)
+        nc.vector.tensor_copy(s2[:].indirect(list1[:, FIRST // 16 : I // 16]), e2[:])
+        last = keep.tile([P, BANK], F32, name="last")
+        nc.gpsimd.tensor_tensor(last[:], s1[:, 3 * BANK : V], olds[3][:], ALU.add)
+
+        backs = []
+        staged = []
+
+        def add_turned(b):
+            for j in range(4):
+                c = b * BANK + j * P
+                nc.tensor.matmul(turned[b][:, j, :], lhsT=s1[:, c : c + P], rhs=ident[:],
+                                 start=False, stop=(j == 3), is_transpose=True)
+            st = keep.tile([P, 4, P], F32, name=f"staged{b}")
+            nc.scalar.copy(out=st[:], in_=turned[b][:])
+            staged.append(st)
+
+        def turn_back(b):
+            bk = psum.tile([P, 4, P], F32, name=f"back{b}", tag=f"bank{4 + b}")
+            for j in range(4):
+                nc.tensor.transpose(bk[:, j, :], staged[b][:, j, :], ident[:])
+            backs.append(bk)
+
+        add_turned(0)
+        for b in range(1, 3):
+            add_turned(b)
+            turn_back(b - 1)
+        turn_back(2)
+        parts = [bk[:].rearrange("p j n -> p (j n)") for bk in backs] + [last[:]]
+
+        for n in range(V // OUT_WIDTH):
+            c = n * OUT_WIDTH
+            b = c // BANK
+            res = keep.tile([P, OUT_WIDTH], F32, name=f"res{n}")
+            part = parts[b][:, c % BANK : c % BANK + OUT_WIDTH]
+            nc.vector.tensor_tensor(res[:], part, s2[:, c : c + OUT_WIDTH], ALU.add)
+            nc.sync.dma_start(out=out[:, c : c + OUT_WIDTH], in_=res[:])

@@ -22,7 +22,7 @@ PACK = 4
 BANK = 512
 SCORE_WIDTHS = (512, 512, 512, 256, 128, 128)
 FIRST = 128
-OUT_WIDTH = 256
+OUT_WIDTHS = (128, 384, 512, 512, 512)
 
 
 def tile_attend_bpairmargin_heads_kernel(tc, hid, voc_words, voc_scales, margin, steep, old, offs, offs2, out):
@@ -64,8 +64,6 @@ def tile_attend_bpairmargin_heads_kernel(tc, hid, voc_words, voc_scales, margin,
 
         ident = keep.tile([P, P], F32, name="ident")
         make_identity(nc, ident[:])
-        s1 = keep.tile([P, V], F32, name="s1")
-        nc.vector.memset(s1[:], 0.0)
 
         mbank = psum.tile([P, PACK, P], F32, name="mbank", tag="bank6")
         for j in range(PACK):
@@ -86,8 +84,9 @@ def tile_attend_bpairmargin_heads_kernel(tc, hid, voc_words, voc_scales, margin,
                 scales=hscale[:, cols],
                 in_=grouped[:, cols, :].rearrange("p q t -> p (q t)"),
             )
-        s2 = keep.tile([P, V], F32, name="s2", tag="late_zero", align_bytes=64)
-        nc.gpsimd.memset(s2[:], 0.0)
+        s1 = keep.tile([P, V], F32, name="s1", tag="late_zero", align_bytes=64)
+        nc.gpsimd.memset(s1[:], 0.0)
+
 
         scores = keep.tile([P, V], F32, name="scores")
         c0 = 0
@@ -110,10 +109,12 @@ def tile_attend_bpairmargin_heads_kernel(tc, hid, voc_words, voc_scales, margin,
                 nc.scalar.copy(out=scores[:, c0 : c0 + width], in_=acc[:])
             c0 = c0 + width
 
+        s2 = keep.tile([P, V], F32, name="s2", tag="words0", align_bytes=64)
+        nc.gpsimd.memset(s2[:], 0.0)
         steep_rows = keep.tile([P, I], F32, name="steep_rows", tag="words1", align_bytes=64)
         nc.scalar.activation(out=steep_rows[:], in_=steep_col[:].to_broadcast([P, I]), func=ACT.Copy)
-        minus_rows = keep.tile([P, FIRST], F32, name="minus_rows")
-        nc.scalar.activation(out=minus_rows[:], in_=steep_rows[:, 0:FIRST], func=ACT.Copy, scale=-1.0)
+        minus_col = keep.tile([P, 1], F32, name="minus_col")
+        nc.scalar.activation(out=minus_col[:], in_=steep_rows[:, 0:1], func=ACT.Copy, scale=-1.0)
 
         turned = []
         for b in range(3):
@@ -130,11 +131,11 @@ def tile_attend_bpairmargin_heads_kernel(tc, hid, voc_words, voc_scales, margin,
         sig = keep.tile([P, I], F32, name="sig")
         for lo, hi in ((0, FIRST), (FIRST, I)):
             nc.scalar.activation(out=sig[:, lo:hi], in_=gap[:, lo:hi], func=ACT.Sigmoid, scale=steep_col[:])
-        e2 = keep.tile([P, I - FIRST], F32, name="e2")
-        nc.scalar.activation(out=e2[:], in_=sig[:, FIRST:I], func=ACT.Copy, scale=minus_rows[:, 0:1])
-        nc.vector.tensor_tensor(s2[:].indirect(list1[:, 0 : FIRST // 16]), sig[:, 0:FIRST], minus_rows[:], ALU.mult)
-        nc.vector.tensor_tensor(s1[:].indirect(list2[:]), sig[:], steep_rows[:], ALU.mult)
-        nc.vector.tensor_copy(s2[:].indirect(list1[:, FIRST // 16 : I // 16]), e2[:])
+        e2 = keep.tile([P, I], F32, name="e2")
+        nc.scalar.activation(out=e2[:], in_=sig[:], func=ACT.Copy, scale=minus_col[:])
+        for lo, hi in ((0, FIRST), (FIRST, I)):
+            nc.vector.tensor_tensor(s1[:].indirect(list2[:, lo // 16 : hi // 16]), sig[:, lo:hi], steep_rows[:, lo:hi], ALU.mult)
+        nc.vector.tensor_copy(s2[:].indirect(list1[:]), e2[:])
         last = keep.tile([P, BANK], F32, name="last")
         nc.gpsimd.tensor_tensor(last[:], s1[:, 3 * BANK : V], olds[3][:], ALU.add)
 
@@ -146,7 +147,7 @@ def tile_attend_bpairmargin_heads_kernel(tc, hid, voc_words, voc_scales, margin,
                 c = b * BANK + j * P
                 nc.tensor.matmul(turned[b][:, j, :], lhsT=s1[:, c : c + P], rhs=ident[:],
                                  start=False, stop=(j == 3), is_transpose=True)
-            st = keep.tile([P, 4, P], F32, name=f"staged{b}")
+            st = keep.tile([P, 4, P], F32, name=f"staged{b}", tag=f"staged{b}")
             nc.scalar.copy(out=st[:], in_=turned[b][:])
             staged.append(st)
 
@@ -156,17 +157,17 @@ def tile_attend_bpairmargin_heads_kernel(tc, hid, voc_words, voc_scales, margin,
                 nc.tensor.transpose(bk[:, j, :], staged[b][:, j, :], ident[:])
             backs.append(bk)
 
-        add_turned(0)
-        for b in range(1, 3):
+        for b in range(3):
             add_turned(b)
-            turn_back(b - 1)
-        turn_back(2)
+        for b in range(3):
+            turn_back(b)
         parts = [bk[:].rearrange("p j n -> p (j n)") for bk in backs] + [last[:]]
 
-        for n in range(V // OUT_WIDTH):
-            c = n * OUT_WIDTH
+        c = 0
+        for n, width in enumerate(OUT_WIDTHS):
             b = c // BANK
-            res = keep.tile([P, OUT_WIDTH], F32, name=f"res{n}")
-            part = parts[b][:, c % BANK : c % BANK + OUT_WIDTH]
-            nc.vector.tensor_tensor(res[:], part, s2[:, c : c + OUT_WIDTH], ALU.add)
-            nc.sync.dma_start(out=out[:, c : c + OUT_WIDTH], in_=res[:])
+            tag = "staged2" if c == 3 * BANK else f"res{n}"
+            res = keep.tile([P, width], F32, name=f"res{n}", tag=tag)
+            nc.vector.tensor_tensor(res[:], parts[b][:, c % BANK : c % BANK + width], s2[:, c : c + width], ALU.add)
+            nc.sync.dma_start(out=out[:, c : c + width], in_=res[:])
+            c = c + width

@@ -22,7 +22,11 @@ PACK = 4
 BANK = 512
 SCORE_WIDTHS = (512, 512, 512, 256, 128, 128)
 FIRST = 128
-OUT_WIDTHS = (128, 384, 512, 512, 512)
+WORD_WIDTHS = (512, 512, 1024)
+TURNED = (4, 4, 2)
+TURN_BANKS = (3, 5, 4)
+BACK_BANKS = (0, 2, 6)
+POOL_WIDTHS = (512, 256)
 
 
 def tile_attend_bpairmargin_heads_kernel(tc, hid, voc_words, voc_scales, margin, steep, old, offs, offs2, out):
@@ -37,42 +41,37 @@ def tile_attend_bpairmargin_heads_kernel(tc, hid, voc_words, voc_scales, margin,
         nc.gpsimd.memset(warm[:, 0:1], 0.0)
 
         raw = keep.tile([P, PACK, Q], F32, name="raw")
-        mcol = keep.tile([P, PACK], F32, name="mcol", tag="codes", align_bytes=64)
-        nc.sync.dma_start(out=mcol[:], in_=margin.rearrange("o (p j) -> (o p) j", j=PACK))
         nc.sync.dma_start(out=raw[:], in_=hid.rearrange("(p t) q -> p t q", t=PACK))
         nc.scalar.activation(out=warm[:, 1:2], in_=warm[:, 0:1], func=ACT.Sigmoid)
         scale_rows = voc_scales[0].bitcast(I32).rearrange("(g r) c -> r g c", r=4)
-        halves = []
-        for h in range(2):
-            words = keep.tile([P, V], U8, name=f"words{h}", tag=f"words{h}", align_bytes=64)
-            nc.sync.dma_start(out=words[:].bitcast(I32), in_=voc_words[0].bitcast(I32)[:, h * 512 : (h + 1) * 512])
-            halves.append(words)
-            if h == 0:
-                for r in range(4):
-                    nc.sync.dma_start(out=plane[:].bitcast(I32)[r:P:32, :], in_=scale_rows[r])
+        for r in range(4):
+            nc.sync.dma_start(out=plane[:].bitcast(I32)[r:P:32, :], in_=scale_rows[r])
+        pieces = []
+        c0 = 0
+        for h, width in enumerate(WORD_WIDTHS):
+            words = keep.tile([P, 2 * width], U8, name=f"words{h}", align_bytes=64)
+            nc.sync.dma_start(out=words[:].bitcast(I32), in_=voc_words[0].bitcast(I32)[:, c0 // 2 : (c0 + width) // 2])
+            pieces.append((c0, width, words))
+            c0 = c0 + width
+        mcol = keep.tile([P, PACK], F32, name="mcol", tag="mcol")
+        nc.sync.dma_start(out=mcol[:], in_=margin.rearrange("o (p j) -> (o p) j", j=PACK))
         list1 = keep.tile([P, I // 16], U16, name="list1")
         nc.sync.dma_start(list1[:], offs)
         list2 = keep.tile([P, I // 16], U16, name="list2")
         nc.sync.dma_start(list2[:], offs2)
         steep_col = keep.tile([P, 1], F32, name="steep_col")
         nc.sync.dma_start(out=steep_col[:], in_=steep)
-        olds = []
-        for b in range(4):
-            old_b = keep.tile([P, BANK], F32, name=f"old{b}")
-            nc.sync.dma_start(out=old_b[:], in_=old[:, b * BANK : (b + 1) * BANK])
-            olds.append(old_b)
+        old_sb = keep.tile([P, V], F32, name="old_sb")
+        nc.sync.dma_start(out=old_sb[:], in_=old)
 
         ident = keep.tile([P, P], F32, name="ident")
         make_identity(nc, ident[:])
-
-        mbank = psum.tile([P, PACK, P], F32, name="mbank", tag="bank6")
-        for j in range(PACK):
-            nc.tensor.transpose(mbank[:, j, :], mcol[:, j : j + 1].to_broadcast([P, P]), ident[:])
-        margin_row = keep.tile([P, I], F32, name="margin_row")
-        nc.scalar.copy(out=margin_row[:].rearrange("p (n j) -> p n j", j=PACK), in_=mbank[:].rearrange("p j n -> p n j"))
+        s1 = keep.tile([P, V], F32, name="s1")
+        nc.vector.memset(s1[:, 0:1280], 0.0)
+        nc.gpsimd.memset(s1[:, 1280:V], 0.0)
 
         grouped = keep.tile([P, Q, PACK], BF16, name="grouped", tag="late_zero", align_bytes=64)
-        codes = keep.tile([P, Q], U32, name="codes", tag="codes", align_bytes=64)
+        codes = keep.tile([P, Q], U32, name="codes", align_bytes=64)
         hscale = keep.tile([P, Q], U8, name="hscale", align_bytes=64)
         for h in range(2):
             cols = slice(h * 64, (h + 1) * 64)
@@ -84,16 +83,15 @@ def tile_attend_bpairmargin_heads_kernel(tc, hid, voc_words, voc_scales, margin,
                 scales=hscale[:, cols],
                 in_=grouped[:, cols, :].rearrange("p q t -> p (q t)"),
             )
-        s1 = keep.tile([P, V], F32, name="s1", tag="late_zero", align_bytes=64)
-        nc.gpsimd.memset(s1[:], 0.0)
-
+        s2 = keep.tile([P, V], F32, name="s2", tag="late_zero", align_bytes=64)
+        nc.gpsimd.memset(s2[:], 0.0)
 
         scores = keep.tile([P, V], F32, name="scores")
         c0 = 0
         for n, width in enumerate(SCORE_WIDTHS):
             acc = psum.tile([P, width], F32, name=f"acc{n}", tag=f"bank{n}")
-            words = halves[c0 // 1024]
-            w0 = 2 * (c0 % 1024)
+            first, words = [(f, t) for f, w, t in pieces if f <= c0 < f + w][0]
+            w0 = 2 * (c0 - first)
             nc.tensor.matmul_mx(
                 out=acc[:],
                 lhsT=codes[:].bitcast(FP8X4),
@@ -109,65 +107,69 @@ def tile_attend_bpairmargin_heads_kernel(tc, hid, voc_words, voc_scales, margin,
                 nc.scalar.copy(out=scores[:, c0 : c0 + width], in_=acc[:])
             c0 = c0 + width
 
-        s2 = keep.tile([P, V], F32, name="s2", tag="words0", align_bytes=64)
-        nc.gpsimd.memset(s2[:], 0.0)
-        steep_rows = keep.tile([P, I], F32, name="steep_rows", tag="words1", align_bytes=64)
+        mbank = psum.tile([P, PACK, P], F32, name="mbank", tag="bank1")
+        for j in range(PACK):
+            nc.tensor.transpose(mbank[:, j, :], mcol[:, j : j + 1].to_broadcast([P, P]), ident[:])
+        margin_row = keep.tile([P, I], F32, name="margin_row")
+        nc.scalar.copy(out=margin_row[:].rearrange("p (n j) -> p n j", j=PACK), in_=mbank[:].rearrange("p j n -> p n j"))
+
+        steep_rows = keep.tile([P, I], F32, name="steep_rows", tag="mcol")
         nc.scalar.activation(out=steep_rows[:], in_=steep_col[:].to_broadcast([P, I]), func=ACT.Copy)
-        minus_col = keep.tile([P, 1], F32, name="minus_col")
-        nc.scalar.activation(out=minus_col[:], in_=steep_rows[:, 0:1], func=ACT.Copy, scale=-1.0)
+        minus_rows = keep.tile([P, FIRST], F32, name="minus_rows")
+        nc.scalar.activation(out=minus_rows[:], in_=steep_rows[:, 0:FIRST], func=ACT.Copy, scale=-1.0)
 
         turned = []
-        for b in range(3):
-            tb = psum.tile([P, 4, P], F32, name=f"turned{b}", tag=f"bank{b}")
-            for j in range(4):
-                nc.tensor.matmul(tb[:, j, :], lhsT=olds[b][:, j * P : (j + 1) * P], rhs=ident[:],
+        for b, blocks in enumerate(TURNED):
+            tb = psum.tile([P, blocks, P], F32, name=f"turned{b}", tag=f"bank{TURN_BANKS[b]}")
+            for j in range(blocks):
+                c = b * BANK + j * P
+                nc.tensor.matmul(tb[:, j, :], lhsT=old_sb[:, c : c + P], rhs=ident[:],
                                  start=(j == 0), stop=False, is_transpose=True)
             turned.append(tb)
 
-        lower = keep.tile([P, I], F32, name="lower")
-        nc.vector.tensor_tensor(lower[:], scores[:].indirect(list1[:]), margin_row[:], ALU.subtract)
+        picked = keep.tile([P, I], F32, name="picked")
+        nc.vector.tensor_copy(picked[:], scores[:].indirect(list1[:]))
+        upper = keep.tile([P, I], F32, name="upper")
+        nc.vector.tensor_tensor(upper[:], scores[:].indirect(list2[:]), margin_row[:], ALU.add)
         gap = keep.tile([P, I], F32, name="gap")
-        nc.vector.tensor_tensor(gap[:], scores[:].indirect(list2[:]), lower[:], ALU.subtract)
         sig = keep.tile([P, I], F32, name="sig")
         for lo, hi in ((0, FIRST), (FIRST, I)):
+            nc.vector.tensor_tensor(gap[:, lo:hi], upper[:, lo:hi], picked[:, lo:hi], ALU.subtract)
             nc.scalar.activation(out=sig[:, lo:hi], in_=gap[:, lo:hi], func=ACT.Sigmoid, scale=steep_col[:])
-        e2 = keep.tile([P, I], F32, name="e2")
-        nc.scalar.activation(out=e2[:], in_=sig[:], func=ACT.Copy, scale=minus_col[:])
-        for lo, hi in ((0, FIRST), (FIRST, I)):
-            nc.vector.tensor_tensor(s1[:].indirect(list2[:, lo // 16 : hi // 16]), sig[:, lo:hi], steep_rows[:, lo:hi], ALU.mult)
-        nc.vector.tensor_copy(s2[:].indirect(list1[:]), e2[:])
-        last = keep.tile([P, BANK], F32, name="last")
-        nc.gpsimd.tensor_tensor(last[:], s1[:, 3 * BANK : V], olds[3][:], ALU.add)
+        e2 = keep.tile([P, I - FIRST], F32, name="e2")
+        nc.scalar.activation(out=e2[:], in_=sig[:, FIRST:I], func=ACT.Copy, scale=minus_rows[:, 0:1])
+        nc.vector.tensor_tensor(s2[:].indirect(list1[:, 0 : FIRST // 16]), sig[:, 0:FIRST], minus_rows[:], ALU.mult)
+        nc.vector.tensor_tensor(s1[:].indirect(list2[:]), sig[:], steep_rows[:], ALU.mult)
+        nc.vector.tensor_copy(s2[:].indirect(list1[:, FIRST // 16 : I // 16]), e2[:])
 
-        backs = []
+        parts = []
+        c = sum(TURNED) * P
+        for n, width in enumerate(POOL_WIDTHS):
+            summed = keep.tile([P, width], F32, name=f"summed{n}")
+            nc.gpsimd.tensor_tensor(summed[:], s1[:, c : c + width], old_sb[:, c : c + width], ALU.add)
+            parts.append((c, width, summed[:]))
+            c = c + width
         staged = []
-
-        def add_turned(b):
-            for j in range(4):
+        for b, blocks in enumerate(TURNED):
+            for j in range(blocks):
                 c = b * BANK + j * P
                 nc.tensor.matmul(turned[b][:, j, :], lhsT=s1[:, c : c + P], rhs=ident[:],
-                                 start=False, stop=(j == 3), is_transpose=True)
-            st = keep.tile([P, 4, P], F32, name=f"staged{b}", tag=f"staged{b}")
+                                 start=False, stop=(j == blocks - 1), is_transpose=True)
+            st = keep.tile([P, blocks, P], F32, name=f"staged{b}")
             nc.scalar.copy(out=st[:], in_=turned[b][:])
             staged.append(st)
-
-        def turn_back(b):
-            bk = psum.tile([P, 4, P], F32, name=f"back{b}", tag=f"bank{4 + b}")
-            for j in range(4):
+        for b, blocks in enumerate(TURNED):
+            bk = psum.tile([P, blocks, P], F32, name=f"back{b}", tag=f"bank{BACK_BANKS[b]}")
+            for j in range(blocks):
                 nc.tensor.transpose(bk[:, j, :], staged[b][:, j, :], ident[:])
-            backs.append(bk)
+            parts.append((b * BANK, blocks * P, bk[:].rearrange("p j n -> p (j n)")))
 
-        for b in range(3):
-            add_turned(b)
-        for b in range(3):
-            turn_back(b)
-        parts = [bk[:].rearrange("p j n -> p (j n)") for bk in backs] + [last[:]]
-
-        c = 0
-        for n, width in enumerate(OUT_WIDTHS):
-            b = c // BANK
-            tag = "staged2" if c == 3 * BANK else f"res{n}"
-            res = keep.tile([P, width], F32, name=f"res{n}", tag=tag)
-            nc.vector.tensor_tensor(res[:], parts[b][:, c % BANK : c % BANK + width], s2[:, c : c + width], ALU.add)
-            nc.sync.dma_start(out=out[:, c : c + width], in_=res[:])
-            c = c + width
+        cuts = ((256, 256), (256,), (256, 256), (256, 256), (256,))
+        for (first, whole, part), widths in zip(parts, cuts):
+            at = 0
+            for width in widths:
+                c = first + at
+                res = keep.tile([P, width], F32, name=f"res{c}")
+                nc.vector.tensor_tensor(res[:], part[:, at : at + width], s2[:, c : c + width], ALU.add)
+                nc.sync.dma_start(out=out[:, c : c + width], in_=res[:])
+                at = at + width

@@ -21,7 +21,7 @@ P = 128
 PACK = 4
 BANK = 512
 SCORE_WIDTHS = (512, 512, 512, 256, 128, 128)
-FIRST = 128
+FIRST = 160
 WORD_WIDTHS = (512, 512, 1024)
 TURNED = (4, 4, 2)
 TURN_BANKS = (3, 5, 4)
@@ -67,8 +67,7 @@ def tile_attend_bpairmargin_heads_kernel(tc, hid, voc_words, voc_scales, margin,
         ident = keep.tile([P, P], F32, name="ident")
         make_identity(nc, ident[:])
         s1 = keep.tile([P, V], F32, name="s1")
-        nc.vector.memset(s1[:, 0:1280], 0.0)
-        nc.gpsimd.memset(s1[:, 1280:V], 0.0)
+        nc.vector.memset(s1[:], 0.0)
 
         grouped = keep.tile([P, Q, PACK], BF16, name="grouped", tag="late_zero", align_bytes=64)
         codes = keep.tile([P, Q], U32, name="codes", align_bytes=64)
@@ -113,10 +112,8 @@ def tile_attend_bpairmargin_heads_kernel(tc, hid, voc_words, voc_scales, margin,
         margin_row = keep.tile([P, I], F32, name="margin_row")
         nc.scalar.copy(out=margin_row[:].rearrange("p (n j) -> p n j", j=PACK), in_=mbank[:].rearrange("p j n -> p n j"))
 
-        steep_rows = keep.tile([P, I], F32, name="steep_rows", tag="mcol")
-        nc.scalar.activation(out=steep_rows[:], in_=steep_col[:].to_broadcast([P, I]), func=ACT.Copy)
-        minus_rows = keep.tile([P, FIRST], F32, name="minus_rows")
-        nc.scalar.activation(out=minus_rows[:], in_=steep_rows[:, 0:FIRST], func=ACT.Copy, scale=-1.0)
+        minus_rows = keep.tile([P, FIRST], F32, name="minus_rows", tag="mcol")
+        nc.scalar.activation(out=minus_rows[:], in_=steep_col[:].to_broadcast([P, FIRST]), func=ACT.Copy, scale=-1.0)
 
         turned = []
         for b, blocks in enumerate(TURNED):
@@ -136,10 +133,12 @@ def tile_attend_bpairmargin_heads_kernel(tc, hid, voc_words, voc_scales, margin,
         for lo, hi in ((0, FIRST), (FIRST, I)):
             nc.vector.tensor_tensor(gap[:, lo:hi], upper[:, lo:hi], picked[:, lo:hi], ALU.subtract)
             nc.scalar.activation(out=sig[:, lo:hi], in_=gap[:, lo:hi], func=ACT.Sigmoid, scale=steep_col[:])
+        db = keep.tile([P, I], F32, name="db")
+        nc.scalar.activation(out=db[:], in_=sig[:], func=ACT.Copy, scale=steep_col[:])
         e2 = keep.tile([P, I - FIRST], F32, name="e2")
         nc.scalar.activation(out=e2[:], in_=sig[:, FIRST:I], func=ACT.Copy, scale=minus_rows[:, 0:1])
         nc.vector.tensor_tensor(s2[:].indirect(list1[:, 0 : FIRST // 16]), sig[:, 0:FIRST], minus_rows[:], ALU.mult)
-        nc.vector.tensor_tensor(s1[:].indirect(list2[:]), sig[:], steep_rows[:], ALU.mult)
+        nc.vector.tensor_copy(s1[:].indirect(list2[:]), db[:])
         nc.vector.tensor_copy(s2[:].indirect(list1[:, FIRST // 16 : I // 16]), e2[:])
 
         parts = []
@@ -164,7 +163,7 @@ def tile_attend_bpairmargin_heads_kernel(tc, hid, voc_words, voc_scales, margin,
                 nc.tensor.transpose(bk[:, j, :], staged[b][:, j, :], ident[:])
             parts.append((b * BANK, blocks * P, bk[:].rearrange("p j n -> p (j n)")))
 
-        cuts = ((256, 256), (256,), (256, 256), (256, 256), (256,))
+        cuts = ((256, 256), (256,), (512,), (512,), (256,))
         for (first, whole, part), widths in zip(parts, cuts):
             at = 0
             for width in widths:

@@ -20,13 +20,17 @@ ACT = mybir.ActivationFunctionType
 P = 128
 PACK = 4
 BANK = 512
-SCORE_WIDTHS = (512, 512, 512, 256, 128, 128)
-FIRST = 160
+GROUP = 16
+
 WORD_WIDTHS = (512, 512, 1024)
-TURNED = (4, 4, 2)
+SCORE_WIDTHS = (512, 512, 512, 256, 128, 128)
+FIRST = 128
+TURNED_BLOCKS = (4, 4, 2)
+POOL_WIDTHS = (512, 256)
+MARGIN_BANK = 1
 TURN_BANKS = (3, 5, 4)
 BACK_BANKS = (0, 2, 6)
-POOL_WIDTHS = (512, 256)
+STORE_WIDTHS = ((256, 256), (256,), (512,), (512,), (256,))
 
 
 def tile_attend_bpairmargin_heads_kernel(tc, hid, voc_words, voc_scales, margin, steep, old, offs, offs2, out):
@@ -35,29 +39,28 @@ def tile_attend_bpairmargin_heads_kernel(tc, hid, voc_words, voc_scales, margin,
         keep = ctx.enter_context(tc.tile_pool(name="keep", bufs=1))
         psum = ctx.enter_context(tc.psum_pool(name="psum", bufs=1))
 
-        plane = keep.tile([P, V], U8, name="plane", align_bytes=64)
-        nc.vector.memset(plane[:].bitcast(I32), 0)
-        warm = keep.tile([P, 2], F32, name="warm")
-        nc.gpsimd.memset(warm[:, 0:1], 0.0)
+        voc_scale_sb = keep.tile([P, V], U8, name="voc_scale_sb", align_bytes=64)
+        nc.vector.memset(voc_scale_sb[:].bitcast(I32), 0)
 
-        raw = keep.tile([P, PACK, Q], F32, name="raw")
-        nc.sync.dma_start(out=raw[:], in_=hid.rearrange("(p t) q -> p t q", t=PACK))
-        nc.scalar.activation(out=warm[:, 1:2], in_=warm[:, 0:1], func=ACT.Sigmoid)
+        hid_sb = keep.tile([P, PACK, Q], F32, name="hid_sb")
+        nc.sync.dma_start(out=hid_sb[:], in_=hid.rearrange("(p t) q -> p t q", t=PACK))
         scale_rows = voc_scales[0].bitcast(I32).rearrange("(g r) c -> r g c", r=4)
         for r in range(4):
-            nc.sync.dma_start(out=plane[:].bitcast(I32)[r:P:32, :], in_=scale_rows[r])
-        pieces = []
-        c0 = 0
-        for h, width in enumerate(WORD_WIDTHS):
-            words = keep.tile([P, 2 * width], U8, name=f"words{h}", align_bytes=64)
-            nc.sync.dma_start(out=words[:].bitcast(I32), in_=voc_words[0].bitcast(I32)[:, c0 // 2 : (c0 + width) // 2])
-            pieces.append((c0, width, words))
-            c0 = c0 + width
-        mcol = keep.tile([P, PACK], F32, name="mcol", tag="mcol")
-        nc.sync.dma_start(out=mcol[:], in_=margin.rearrange("o (p j) -> (o p) j", j=PACK))
-        list1 = keep.tile([P, I // 16], U16, name="list1")
+            nc.sync.dma_start(out=voc_scale_sb[:].bitcast(I32)[r:P:32, :], in_=scale_rows[r])
+        word_tiles = []
+        first = 0
+        for n, width in enumerate(WORD_WIDTHS):
+            words = keep.tile([P, 2 * width], U8, name=f"words{n}", align_bytes=64)
+            nc.sync.dma_start(
+                out=words[:].bitcast(I32), in_=voc_words[0].bitcast(I32)[:, first // 2 : (first + width) // 2]
+            )
+            word_tiles.append((first, width, words))
+            first = first + width
+        margin_cols = keep.tile([P, I // P], F32, name="margin_cols")
+        nc.sync.dma_start(out=margin_cols[:], in_=margin.rearrange("o (p j) -> (o p) j", j=I // P))
+        list1 = keep.tile([P, I // GROUP], U16, name="list1")
         nc.sync.dma_start(list1[:], offs)
-        list2 = keep.tile([P, I // 16], U16, name="list2")
+        list2 = keep.tile([P, I // GROUP], U16, name="list2")
         nc.sync.dma_start(list2[:], offs2)
         steep_col = keep.tile([P, 1], F32, name="steep_col")
         nc.sync.dma_start(out=steep_col[:], in_=steep)
@@ -69,106 +72,114 @@ def tile_attend_bpairmargin_heads_kernel(tc, hid, voc_words, voc_scales, margin,
         s1 = keep.tile([P, V], F32, name="s1")
         nc.vector.memset(s1[:], 0.0)
 
-        grouped = keep.tile([P, Q, PACK], BF16, name="grouped", tag="late_zero", align_bytes=64)
-        codes = keep.tile([P, Q], U32, name="codes", align_bytes=64)
-        hscale = keep.tile([P, Q], U8, name="hscale", align_bytes=64)
-        for h in range(2):
-            cols = slice(h * 64, (h + 1) * 64)
-            nc.vector.tensor_copy(out=grouped[:, cols, :], in_=raw[:, :, cols].rearrange("p t q -> p q t"))
-        for h in range(2):
-            cols = slice(h * 64, (h + 1) * 64)
+        grouped = keep.tile([P, Q, PACK], BF16, name="grouped", tag="grouped_then_s2", align_bytes=64)
+        hid_codes = keep.tile([P, Q], U32, name="hid_codes", align_bytes=64)
+        hid_scales = keep.tile([P, Q], U8, name="hid_scales", align_bytes=64)
+        halves = (slice(0, Q // 2), slice(Q // 2, Q))
+        for cols in halves:
+            nc.vector.tensor_copy(out=grouped[:, cols, :], in_=hid_sb[:, :, cols].rearrange("p t q -> p q t"))
+        for cols in halves:
             nc.vector.quantize_mx(
-                out=codes[:, cols].bitcast(FP8X4),
-                scales=hscale[:, cols],
+                out=hid_codes[:, cols].bitcast(FP8X4),
+                scales=hid_scales[:, cols],
                 in_=grouped[:, cols, :].rearrange("p q t -> p (q t)"),
             )
-        s2 = keep.tile([P, V], F32, name="s2", tag="late_zero", align_bytes=64)
+        s2 = keep.tile([P, V], F32, name="s2", tag="grouped_then_s2", align_bytes=64)
         nc.gpsimd.memset(s2[:], 0.0)
 
         scores = keep.tile([P, V], F32, name="scores")
-        c0 = 0
+        c = 0
         for n, width in enumerate(SCORE_WIDTHS):
             acc = psum.tile([P, width], F32, name=f"acc{n}", tag=f"bank{n}")
-            first, words = [(f, t) for f, w, t in pieces if f <= c0 < f + w][0]
-            w0 = 2 * (c0 - first)
+            first, words = [(f, t) for f, w, t in word_tiles if f <= c < f + w][0]
+            byte = 2 * (c - first)
             nc.tensor.matmul_mx(
                 out=acc[:],
-                lhsT=codes[:].bitcast(FP8X4),
-                lhsT_scale=hscale[:],
-                rhs=words[:, w0 : w0 + 2 * width].bitcast(FP4X4),
-                rhs_scale=plane[:, c0 : c0 + width],
+                lhsT=hid_codes[:].bitcast(FP8X4),
+                lhsT_scale=hid_scales[:],
+                rhs=words[:, byte : byte + 2 * width].bitcast(FP4X4),
+                rhs_scale=voc_scale_sb[:, c : c + width],
                 start=True,
                 stop=True,
             )
             if n % 2 == 0:
-                nc.vector.tensor_copy(out=scores[:, c0 : c0 + width], in_=acc[:])
+                nc.vector.tensor_copy(out=scores[:, c : c + width], in_=acc[:])
             else:
-                nc.scalar.copy(out=scores[:, c0 : c0 + width], in_=acc[:])
-            c0 = c0 + width
+                nc.scalar.copy(out=scores[:, c : c + width], in_=acc[:])
+            c = c + width
 
-        mbank = psum.tile([P, PACK, P], F32, name="mbank", tag="bank1")
-        for j in range(PACK):
-            nc.tensor.transpose(mbank[:, j, :], mcol[:, j : j + 1].to_broadcast([P, P]), ident[:])
-        margin_row = keep.tile([P, I], F32, name="margin_row")
-        nc.scalar.copy(out=margin_row[:].rearrange("p (n j) -> p n j", j=PACK), in_=mbank[:].rearrange("p j n -> p n j"))
+        margin_ps = psum.tile([P, I // P, P], F32, name="margin_ps", tag=f"bank{MARGIN_BANK}")
+        for j in range(I // P):
+            nc.tensor.transpose(margin_ps[:, j, :], margin_cols[:, j : j + 1].to_broadcast([P, P]), ident[:])
+        margin_rows = keep.tile([P, I], F32, name="margin_rows")
+        nc.scalar.copy(
+            out=margin_rows[:].rearrange("p (n j) -> p n j", j=I // P), in_=margin_ps[:].rearrange("p j n -> p n j")
+        )
 
-        minus_rows = keep.tile([P, FIRST], F32, name="minus_rows", tag="mcol")
-        nc.scalar.activation(out=minus_rows[:], in_=steep_col[:].to_broadcast([P, FIRST]), func=ACT.Copy, scale=-1.0)
+        steep_rows = keep.tile([P, I], F32, name="steep_rows")
+        nc.gpsimd.tensor_scalar(steep_rows[:], steep_col[:].to_broadcast([P, I]), 1.0, 0.0, ALU.mult, ALU.add)
+        minus_rows = keep.tile([P, FIRST], F32, name="minus_rows")
+        nc.gpsimd.tensor_scalar(minus_rows[:], steep_col[:].to_broadcast([P, FIRST]), -1.0, 0.0, ALU.mult, ALU.add)
 
         turned = []
-        for b, blocks in enumerate(TURNED):
-            tb = psum.tile([P, blocks, P], F32, name=f"turned{b}", tag=f"bank{TURN_BANKS[b]}")
+        for b, blocks in enumerate(TURNED_BLOCKS):
+            bank = psum.tile([P, blocks, P], F32, name=f"turned{b}", tag=f"bank{TURN_BANKS[b]}")
             for j in range(blocks):
                 c = b * BANK + j * P
-                nc.tensor.matmul(tb[:, j, :], lhsT=old_sb[:, c : c + P], rhs=ident[:],
-                                 start=(j == 0), stop=False, is_transpose=True)
-            turned.append(tb)
+                nc.tensor.matmul(
+                    bank[:, j, :], lhsT=old_sb[:, c : c + P], rhs=ident[:], start=(j == 0), stop=False, is_transpose=True
+                )
+            turned.append(bank)
 
         picked = keep.tile([P, I], F32, name="picked")
         nc.vector.tensor_copy(picked[:], scores[:].indirect(list1[:]))
         upper = keep.tile([P, I], F32, name="upper")
-        nc.vector.tensor_tensor(upper[:], scores[:].indirect(list2[:]), margin_row[:], ALU.add)
+        nc.vector.tensor_tensor(upper[:], scores[:].indirect(list2[:]), margin_rows[:], ALU.add)
         gap = keep.tile([P, I], F32, name="gap")
         sig = keep.tile([P, I], F32, name="sig")
-        for lo, hi in ((0, FIRST), (FIRST, I)):
-            nc.vector.tensor_tensor(gap[:, lo:hi], upper[:, lo:hi], picked[:, lo:hi], ALU.subtract)
-            nc.scalar.activation(out=sig[:, lo:hi], in_=gap[:, lo:hi], func=ACT.Sigmoid, scale=steep_col[:])
-        db = keep.tile([P, I], F32, name="db")
-        nc.scalar.activation(out=db[:], in_=sig[:], func=ACT.Copy, scale=steep_col[:])
-        e2 = keep.tile([P, I - FIRST], F32, name="e2")
-        nc.scalar.activation(out=e2[:], in_=sig[:, FIRST:I], func=ACT.Copy, scale=minus_rows[:, 0:1])
-        nc.vector.tensor_tensor(s2[:].indirect(list1[:, 0 : FIRST // 16]), sig[:, 0:FIRST], minus_rows[:], ALU.mult)
-        nc.vector.tensor_copy(s1[:].indirect(list2[:]), db[:])
-        nc.vector.tensor_copy(s2[:].indirect(list1[:, FIRST // 16 : I // 16]), e2[:])
+        for slots in (slice(0, FIRST), slice(FIRST, I)):
+            nc.vector.tensor_tensor(gap[:, slots], upper[:, slots], picked[:, slots], ALU.subtract)
+            nc.scalar.activation(out=sig[:, slots], in_=gap[:, slots], func=ACT.Sigmoid, scale=steep_col[:])
+        e2_rest = keep.tile([P, I - FIRST], F32, name="e2_rest")
+        nc.scalar.activation(out=e2_rest[:], in_=sig[:, FIRST:I], func=ACT.Copy, scale=minus_rows[:, 0:1])
 
-        parts = []
-        c = sum(TURNED) * P
+        nc.vector.tensor_tensor(s2[:].indirect(list1[:, 0 : FIRST // GROUP]), sig[:, 0:FIRST], minus_rows[:], ALU.mult)
+        nc.vector.tensor_tensor(s1[:].indirect(list2[:]), sig[:], steep_rows[:], ALU.mult)
+        nc.vector.tensor_copy(s2[:].indirect(list1[:, FIRST // GROUP : I // GROUP]), e2_rest[:])
+
+        pieces = []
+        c = sum(TURNED_BLOCKS) * P
         for n, width in enumerate(POOL_WIDTHS):
             summed = keep.tile([P, width], F32, name=f"summed{n}")
             nc.gpsimd.tensor_tensor(summed[:], s1[:, c : c + width], old_sb[:, c : c + width], ALU.add)
-            parts.append((c, width, summed[:]))
+            pieces.append((c, summed[:]))
             c = c + width
         staged = []
-        for b, blocks in enumerate(TURNED):
+        for b, blocks in enumerate(TURNED_BLOCKS):
             for j in range(blocks):
                 c = b * BANK + j * P
-                nc.tensor.matmul(turned[b][:, j, :], lhsT=s1[:, c : c + P], rhs=ident[:],
-                                 start=False, stop=(j == blocks - 1), is_transpose=True)
-            st = keep.tile([P, blocks, P], F32, name=f"staged{b}")
-            nc.scalar.copy(out=st[:], in_=turned[b][:])
-            staged.append(st)
-        for b, blocks in enumerate(TURNED):
-            bk = psum.tile([P, blocks, P], F32, name=f"back{b}", tag=f"bank{BACK_BANKS[b]}")
+                nc.tensor.matmul(
+                    turned[b][:, j, :],
+                    lhsT=s1[:, c : c + P],
+                    rhs=ident[:],
+                    start=False,
+                    stop=(j == blocks - 1),
+                    is_transpose=True,
+                )
+            sums = keep.tile([P, blocks, P], F32, name=f"staged{b}")
+            nc.scalar.copy(out=sums[:], in_=turned[b][:])
+            staged.append(sums)
+        for b, blocks in enumerate(TURNED_BLOCKS):
+            back = psum.tile([P, blocks, P], F32, name=f"back{b}", tag=f"bank{BACK_BANKS[b]}")
             for j in range(blocks):
-                nc.tensor.transpose(bk[:, j, :], staged[b][:, j, :], ident[:])
-            parts.append((b * BANK, blocks * P, bk[:].rearrange("p j n -> p (j n)")))
+                nc.tensor.transpose(back[:, j, :], staged[b][:, j, :], ident[:])
+            pieces.append((b * BANK, back[:].rearrange("p j n -> p (j n)")))
 
-        cuts = ((256, 256), (256,), (512,), (512,), (256,))
-        for (first, whole, part), widths in zip(parts, cuts):
+        for (first, piece), widths in zip(pieces, STORE_WIDTHS):
             at = 0
             for width in widths:
                 c = first + at
-                res = keep.tile([P, width], F32, name=f"res{c}")
-                nc.vector.tensor_tensor(res[:], part[:, at : at + width], s2[:, c : c + width], ALU.add)
-                nc.sync.dma_start(out=out[:, c : c + width], in_=res[:])
+                result = keep.tile([P, width], F32, name=f"result{c}")
+                nc.vector.tensor_tensor(result[:], piece[:, at : at + width], s2[:, c : c + width], ALU.add)
+                nc.sync.dma_start(out=out[:, c : c + width], in_=result[:])
                 at = at + width

from contextlib import ExitStack

import concourse.mybir as mybir
from concourse.masks import make_identity

D, V, Q, I = 512, 2048, 128, 512
FLOPS = 2 * D * V * Q

F32 = mybir.dt.float32
BF16 = mybir.dt.bfloat16
I32 = mybir.dt.int32
U32 = mybir.dt.uint32
U16 = mybir.dt.uint16
U8 = mybir.dt.uint8
FP8X4 = mybir.dt.float8_e4m3fn_x4
FP4X4 = mybir.dt.float4_e2m1fn_x4
ALU = mybir.AluOpType
ACT = mybir.ActivationFunctionType

P = 128
PACK = 4
BANK = 512
GROUP = 16

WORD_WIDTHS = (512, 512, 1024)
SCORE_WIDTHS = (512, 512, 512, 256, 128, 128)
FIRST = 128
TURNED_BLOCKS = (4, 4, 2)
POOL_WIDTHS = (512, 256)
MARGIN_BANK = 1
TURN_BANKS = (3, 5, 4)
BACK_BANKS = (0, 2, 6)
STORE_WIDTHS = ((256, 256), (256,), (512,), (512,), (256,))


def tile_attend_bpairmargin_heads_kernel(tc, hid, voc_words, voc_scales, margin, steep, old, offs, offs2, out):
    nc = tc.nc
    with ExitStack() as ctx:
        keep = ctx.enter_context(tc.tile_pool(name="keep", bufs=1))
        psum = ctx.enter_context(tc.psum_pool(name="psum", bufs=1))

        voc_scale_sb = keep.tile([P, V], U8, name="voc_scale_sb", align_bytes=64)
        nc.vector.memset(voc_scale_sb[:].bitcast(I32), 0)

        hid_sb = keep.tile([P, PACK, Q], F32, name="hid_sb")
        nc.sync.dma_start(out=hid_sb[:], in_=hid.rearrange("(p t) q -> p t q", t=PACK))
        scale_rows = voc_scales[0].bitcast(I32).rearrange("(g r) c -> r g c", r=4)
        for r in range(4):
            nc.sync.dma_start(out=voc_scale_sb[:].bitcast(I32)[r:P:32, :], in_=scale_rows[r])
        word_tiles = []
        first = 0
        for n, width in enumerate(WORD_WIDTHS):
            words = keep.tile([P, 2 * width], U8, name=f"words{n}", align_bytes=64)
            nc.sync.dma_start(
                out=words[:].bitcast(I32), in_=voc_words[0].bitcast(I32)[:, first // 2 : (first + width) // 2]
            )
            word_tiles.append((first, width, words))
            first = first + width
        margin_cols = keep.tile([P, I // P], F32, name="margin_cols")
        nc.sync.dma_start(out=margin_cols[:], in_=margin.rearrange("o (p j) -> (o p) j", j=I // P))
        list1 = keep.tile([P, I // GROUP], U16, name="list1")
        nc.sync.dma_start(list1[:], offs)
        list2 = keep.tile([P, I // GROUP], U16, name="list2")
        nc.sync.dma_start(list2[:], offs2)
        steep_col = keep.tile([P, 1], F32, name="steep_col")
        nc.sync.dma_start(out=steep_col[:], in_=steep)
        old_sb = keep.tile([P, V], F32, name="old_sb")
        nc.sync.dma_start(out=old_sb[:], in_=old)

        ident = keep.tile([P, P], F32, name="ident")
        make_identity(nc, ident[:])
        s1 = keep.tile([P, V], F32, name="s1")
        nc.vector.memset(s1[:], 0.0)

        grouped = keep.tile([P, Q, PACK], BF16, name="grouped", tag="grouped_then_s2", align_bytes=64)
        hid_codes = keep.tile([P, Q], U32, name="hid_codes", align_bytes=64)
        hid_scales = keep.tile([P, Q], U8, name="hid_scales", align_bytes=64)
        halves = (slice(0, Q // 2), slice(Q // 2, Q))
        for cols in halves:
            nc.vector.tensor_copy(out=grouped[:, cols, :], in_=hid_sb[:, :, cols].rearrange("p t q -> p q t"))
        for cols in halves:
            nc.vector.quantize_mx(
                out=hid_codes[:, cols].bitcast(FP8X4),
                scales=hid_scales[:, cols],
                in_=grouped[:, cols, :].rearrange("p q t -> p (q t)"),
            )
        s2 = keep.tile([P, V], F32, name="s2", tag="grouped_then_s2", align_bytes=64)
        nc.gpsimd.memset(s2[:], 0.0)

        scores = keep.tile([P, V], F32, name="scores")
        c = 0
        for n, width in enumerate(SCORE_WIDTHS):
            acc = psum.tile([P, width], F32, name=f"acc{n}", tag=f"bank{n}")
            first, words = [(f, t) for f, w, t in word_tiles if f <= c < f + w][0]
            byte = 2 * (c - first)
            nc.tensor.matmul_mx(
                out=acc[:],
                lhsT=hid_codes[:].bitcast(FP8X4),
                lhsT_scale=hid_scales[:],
                rhs=words[:, byte : byte + 2 * width].bitcast(FP4X4),
                rhs_scale=voc_scale_sb[:, c : c + width],
                start=True,
                stop=True,
            )
            if n % 2 == 0:
                nc.vector.tensor_copy(out=scores[:, c : c + width], in_=acc[:])
            else:
                nc.scalar.copy(out=scores[:, c : c + width], in_=acc[:])
            c = c + width

        margin_ps = psum.tile([P, I // P, P], F32, name="margin_ps", tag=f"bank{MARGIN_BANK}")
        for j in range(I // P):
            nc.tensor.transpose(margin_ps[:, j, :], margin_cols[:, j : j + 1].to_broadcast([P, P]), ident[:])
        margin_rows = keep.tile([P, I], F32, name="margin_rows")
        nc.scalar.copy(
            out=margin_rows[:].rearrange("p (n j) -> p n j", j=I // P), in_=margin_ps[:].rearrange("p j n -> p n j")
        )

        steep_rows = keep.tile([P, I], F32, name="steep_rows")
        nc.gpsimd.tensor_scalar(steep_rows[:], steep_col[:].to_broadcast([P, I]), 1.0, 0.0, ALU.mult, ALU.add)
        minus_rows = keep.tile([P, FIRST], F32, name="minus_rows")
        nc.gpsimd.tensor_scalar(minus_rows[:], steep_col[:].to_broadcast([P, FIRST]), -1.0, 0.0, ALU.mult, ALU.add)

        turned = []
        for b, blocks in enumerate(TURNED_BLOCKS):
            bank = psum.tile([P, blocks, P], F32, name=f"turned{b}", tag=f"bank{TURN_BANKS[b]}")
            for j in range(blocks):
                c = b * BANK + j * P
                nc.tensor.matmul(
                    bank[:, j, :], lhsT=old_sb[:, c : c + P], rhs=ident[:], start=(j == 0), stop=False, is_transpose=True
                )
            turned.append(bank)

        picked = keep.tile([P, I], F32, name="picked")
        nc.vector.tensor_copy(picked[:], scores[:].indirect(list1[:]))
        upper = keep.tile([P, I], F32, name="upper")
        nc.vector.tensor_tensor(upper[:], scores[:].indirect(list2[:]), margin_rows[:], ALU.add)
        gap = keep.tile([P, I], F32, name="gap")
        sig = keep.tile([P, I], F32, name="sig")
        for slots in (slice(0, FIRST), slice(FIRST, I)):
            nc.vector.tensor_tensor(gap[:, slots], upper[:, slots], picked[:, slots], ALU.subtract)
            nc.scalar.activation(out=sig[:, slots], in_=gap[:, slots], func=ACT.Sigmoid, scale=steep_col[:])
        e2_rest = keep.tile([P, I - FIRST], F32, name="e2_rest")
        nc.scalar.activation(out=e2_rest[:], in_=sig[:, FIRST:I], func=ACT.Copy, scale=minus_rows[:, 0:1])

        nc.vector.tensor_tensor(s2[:].indirect(list1[:, 0 : FIRST // GROUP]), sig[:, 0:FIRST], minus_rows[:], ALU.mult)
        nc.vector.tensor_tensor(s1[:].indirect(list2[:]), sig[:], steep_rows[:], ALU.mult)
        nc.vector.tensor_copy(s2[:].indirect(list1[:, FIRST // GROUP : I // GROUP]), e2_rest[:])

        pieces = []
        c = sum(TURNED_BLOCKS) * P
        for n, width in enumerate(POOL_WIDTHS):
            summed = keep.tile([P, width], F32, name=f"summed{n}")
            nc.gpsimd.tensor_tensor(summed[:], s1[:, c : c + width], old_sb[:, c : c + width], ALU.add)
            pieces.append((c, summed[:]))
            c = c + width
        staged = []
        for b, blocks in enumerate(TURNED_BLOCKS):
            for j in range(blocks):
                c = b * BANK + j * P
                nc.tensor.matmul(
                    turned[b][:, j, :],
                    lhsT=s1[:, c : c + P],
                    rhs=ident[:],
                    start=False,
                    stop=(j == blocks - 1),
                    is_transpose=True,
                )
            sums = keep.tile([P, blocks, P], F32, name=f"staged{b}")
            nc.scalar.copy(out=sums[:], in_=turned[b][:])
            staged.append(sums)
        for b, blocks in enumerate(TURNED_BLOCKS):
            back = psum.tile([P, blocks, P], F32, name=f"back{b}", tag=f"bank{BACK_BANKS[b]}")
            for j in range(blocks):
                nc.tensor.transpose(back[:, j, :], staged[b][:, j, :], ident[:])
            pieces.append((b * BANK, back[:].rearrange("p j n -> p (j n)")))

        for (first, piece), widths in zip(pieces, STORE_WIDTHS):
            at = 0
            for width in widths:
                c = first + at
                result = keep.tile([P, width], F32, name=f"result{c}")
                nc.vector.tensor_tensor(result[:], piece[:, at : at + width], s2[:, c : c + width], ALU.add)
                nc.sync.dma_start(out=out[:, c : c + width], in_=result[:])
                at = at + width
